import numpy as np
import ml_dtypes


def mxq(x, axis, fmt="e4m3"):
    dtype, down = {"e4m3": (ml_dtypes.float8_e4m3fn, 7), "e5m2": (ml_dtypes.float8_e5m2, 14)}[fmt]
    v = np.moveaxis(np.asarray(x, np.float32).astype(ml_dtypes.bfloat16).astype(np.float64), axis, -1)
    blocks = v.reshape(v.shape[:-1] + (-1, 32))
    amax = np.abs(blocks).max(-1, keepdims=True)
    byte = np.maximum(np.where(amax > 0, np.frexp(amax)[1] - 1 + 127, 0) - down, 1)
    scale = np.exp2(byte - 127.0)
    codes = (blocks / scale).astype(np.float32).astype(dtype).astype(np.float64)
    return np.moveaxis((codes * scale).reshape(v.shape), -1, axis)


WIDE = False


def mx_kscale(k):
    if not WIDE:
        return np.ones(k)
    levels = np.array([10, -10, 5, -5, 0])
    if k % 512:
        return np.exp2(np.random.permutation(np.resize(levels, k // 32))).repeat(32)
    a = np.empty((k // 512, 16))
    for p in range(k // 512):
        a[p, :8] = np.random.permutation(np.resize(levels, 8))
        for g in range(8):
            far = levels[np.abs(levels - a[p, g]) >= 10]
            a[p, g + 8] = far[np.random.randint(len(far))]
    return np.exp2(a.ravel()).repeat(32)


BF16 = ml_dtypes.bfloat16


def bf(x):
    return np.asarray(x, np.float32).astype(BF16)


def f64(x):
    return np.asarray(x).astype(np.float64)


E2M1 = np.array([0.0, 0.5, 1.0, 1.5, 2.0, 3.0, 4.0, 6.0, -0.0, -0.5, -1.0, -1.5, -2.0, -3.0, -4.0, -6.0])


def pack_weight(w, fmt):
    k, n = w.shape
    w = f64(bf(w)).reshape(k // 32, 32, n)
    amax = np.abs(w).max(1)
    if fmt == "e4m3":
        byte = np.frexp(amax)[1] - 1 + 127 - 7
    else:
        mant, ex = np.frexp(amax / 6.0)
        byte = np.where(mant > 0.5, ex, ex - 1) + 127
    byte = np.clip(np.where(amax > 0, byte, 1), 1, 254)
    scaled = (w * np.exp2(127.0 - byte)[:, None, :]).reshape(k, n).astype(np.float32)
    by_word = np.ascontiguousarray(scaled.reshape(k // 512, 128, 4, n).transpose(0, 1, 3, 2))
    if fmt == "e4m3":
        words = by_word.astype(ml_dtypes.float8_e4m3fn).view(np.uint8)
    else:
        c = by_word.astype(ml_dtypes.float4_e2m1fn).view(np.uint8) & 0xF
        words = c[..., 0::2] | (c[..., 1::2] << 4)
    return np.ascontiguousarray(words), np.ascontiguousarray(byte.astype(np.uint8).reshape(k // 512, 16, n))


def unpack_weight(words, scales, fmt):
    g, p, n, _ = words.shape
    if fmt == "e4m3":
        vals = np.ascontiguousarray(words).view(ml_dtypes.float8_e4m3fn).astype(np.float64)
    else:
        nib = np.empty((g, p, n, 4), np.uint8)
        nib[..., 0::2] = words & 0xF
        nib[..., 1::2] = words >> 4
        vals = E2M1[nib]
    vals = vals * np.repeat(np.exp2(scales.astype(np.float64) - 127.0), 8, axis=1)[..., None]
    return vals.transpose(0, 1, 3, 2).reshape(g * 512, n)

def planes(Y):
    n, m = Y.shape
    b = f64(bf(Y)).reshape(n // 32, 32, m)
    amax = np.abs(b).max(1)
    byte = np.clip(np.where(amax > 0, np.frexp(amax)[1] - 1 + 127 - 7, 1), 1, 254)
    codes = (b * np.exp2(127.0 - byte)[:, None, :]).reshape(n, m).astype(np.float32).astype(ml_dtypes.float8_e4m3fn).view(np.uint8)
    words = codes.reshape(n // 512, 128, 4, m).transpose(0, 1, 3, 2)
    return np.ascontiguousarray(words), np.ascontiguousarray(byte.astype(np.uint8).reshape(n // 512, 16, m))


T, D, F, E, R = 1024, 1024, 1024, 128, 512


def softmax_last(l):
    m = np.max(l, axis=-1, keepdims=True)
    p = np.exp(l - m)
    return p / np.sum(p, axis=-1, keepdims=True)


def setup_inputs():
    s, t = mx_kscale(D), mx_kscale(R)
    sd, sr = np.sqrt(D), np.sqrt(R)
    x = bf(np.random.standard_normal((T, D)) * s)
    w0_words, w0_scales = pack_weight(np.random.standard_normal((D, F)) / sd / s[:, None], "e4m3")
    wr_words, wr_scales = pack_weight(np.random.standard_normal((D, E)) / sd / s[:, None], "e4m3")
    br = bf(np.random.standard_normal(E) * 0.5)
    a_words, a_scales = pack_weight(np.random.standard_normal((D, R)) / sd / s[:, None] * t, "e4m3")
    b_words, b_scales = pack_weight(np.random.standard_normal((R, F)) * 0.6 / sr / t[:, None], "e4m3")
    return {
        "x": x,
        "w0_words": w0_words,
        "w0_scales": w0_scales,
        "wr_words": wr_words,
        "wr_scales": wr_scales,
        "br": br,
        "a_words": a_words,
        "a_scales": a_scales,
        "b_words": b_words,
        "b_scales": b_scales,
    }


def core(x, w0_words, w0_scales, wr_words, wr_scales, br, a_words, a_scales, b_words, b_scales):
    w0 = unpack_weight(w0_words, w0_scales, "e4m3")
    wr = unpack_weight(wr_words, wr_scales, "e4m3")
    a = unpack_weight(a_words, a_scales, "e4m3")
    b = unpack_weight(b_words, b_scales, "e4m3")
    n_tok = x.shape[0]
    n_exp = wr.shape[1]
    rank = a.shape[1]
    per_exp = rank // n_exp
    xq = mxq(f64(x), 1, "e4m3")
    l = (xq @ wr) + f64(br)
    g = float(n_exp) * softmax_last(l)
    u = xq @ a
    z = u.reshape(n_tok, n_exp, per_exp) * g[:, :, None]
    z = z.reshape(n_tok, rank)
    y = (xq @ w0) + (mxq(z, 1, "e4m3") @ b)
    return y


def reference(x, w0_words, w0_scales, wr_words, wr_scales, br, a_words, a_scales, b_words, b_scales):
    R_out = core(x, w0_words, w0_scales, wr_words, wr_scales, br, a_words, a_scales, b_words, b_scales)
    words, scales = planes(R_out.T)
    return R_out, words, scales

@@ -1,0 +1,519 @@
+from contextlib import ExitStack
+
+import concourse.mybir as mybir
+from concourse.masks import make_identity
+
+T, D, F, E, R = 1024, 1024, 1024, 128, 512
+FLOPS = 2 * T * (D * F + D * E + D * R + R * F)
+
+F32 = mybir.dt.float32
+BF16 = mybir.dt.bfloat16
+I32 = mybir.dt.int32
+U32 = mybir.dt.uint32
+U8 = mybir.dt.uint8
+FP8X4 = mybir.dt.float8_e4m3fn_x4
+ALU = mybir.AluOpType
+ACT = mybir.ActivationFunctionType
+AX = mybir.AxisListType
+
+P = 128
+TILES = T // P
+
+
+def tile_rankwisemoloradenserouter_x2_kernel(
+    tc, x, w0_words, w0_scales, wr_words, wr_scales, br, a_words, a_scales, b_words, b_scales,
+    out_0, out_1, out_2,
+):
+    nc = tc.nc
+    with ExitStack() as ctx:
+        const = ctx.enter_context(tc.tile_pool(name="const", bufs=1))
+        keep = ctx.enter_context(tc.tile_pool(name="keep", bufs=TILES))
+        four = ctx.enter_context(tc.tile_pool(name="four", bufs=4))
+        psum_t = ctx.enter_context(tc.psum_pool(name="psum_t", bufs=3))
+        psum_u = ctx.enter_context(tc.psum_pool(name="psum_u", bufs=2))
+        psum_y = ctx.enter_context(tc.psum_pool(name="psum_y", bufs=3))
+        ctx.enter_context(tc.manual_schedule())
+
+        ident = const.tile([P, P], F32, name="ident")
+        ones = const.tile([P, P], BF16, name="ones", align_bytes=64)
+        br_row = const.tile([P, E], BF16, name="br_row", align_bytes=64)
+        br_all = const.tile([P, E], F32, name="br_all")
+        warm = const.tile([P, 1], F32, name="warm")
+        w0_c = const.tile([P, 2, F], U32, name="w0_c", align_bytes=64)
+        w0_s = const.tile([P, 2, F], U8, name="w0_s", align_bytes=64)
+        wr_c = const.tile([P, 2, E], U32, name="wr_c", align_bytes=64)
+        wr_s = const.tile([P, 2, E], U8, name="wr_s", align_bytes=64)
+        a_c = const.tile([P, 2, R], U32, name="a_c", align_bytes=64)
+        a_s = const.tile([P, 2, R], U8, name="a_s", align_bytes=64)
+        b_c = const.tile([P, 1, F], U32, name="b_c", align_bytes=64)
+        b_s = const.tile([P, 1, F], U8, name="b_s", align_bytes=64)
+        y_s = const.tile([P, 2, 6 * P], U8, name="y_s", align_bytes=64)
+        y_s2 = const.tile([P, 2, 2 * P], U8, name="y_s2", align_bytes=64)
+
+        xs, xd, xg, xc, xp, xt_ps = {}, {}, {}, {}, {}, {}
+        lt, ln, mn, sm, pe, rc = {}, {}, {}, {}, {}, {}
+        ups, zb, zt_ps, zg, zc, zs = {}, {}, {}, {}, {}, {}
+        yps, yo, yb, yt_ps, yg, yc = {}, {}, {}, {}, {}, {}
+
+        def load_x(lo, hi):
+            tiles = const.tile([P, hi - lo, D], BF16, name="x_in%d" % lo, align_bytes=64)
+            nc.sync.dma_start(out=tiles[:], in_=x[P * lo : P * hi, :].rearrange("(i p) d -> p i d", p=P))
+            for i in range(lo, hi):
+                xs[i] = tiles[:, i - lo, :]
+
+        def load_words(dst, src, g=None):
+            if g is None:
+                nc.sync.dma_start(
+                    out=dst[:].bitcast(I32), in_=src.rearrange("g p n t -> p g (n t)").bitcast(I32)
+                )
+            else:
+                nc.sync.dma_start(
+                    out=dst[:, g, :].bitcast(I32), in_=src[g].rearrange("p n t -> p (n t)").bitcast(I32)
+                )
+
+        def load_scales(queue, dst, src):
+            for q in range(4):
+                queue.dma_start(
+                    out=dst[32 * q : 32 * q + 4].bitcast(I32),
+                    in_=src[:, 4 * q : 4 * q + 4, :].rearrange("g r n -> r g n").bitcast(I32),
+                )
+
+        nc.vector.memset(br_row[:], 0.0)
+        nc.vector.memset(wr_s[:].rearrange("p g n -> p (g n)").bitcast(I32), 0)
+        nc.vector.memset(a_s[:].rearrange("p g n -> p (g n)").bitcast(I32), 0)
+        nc.vector.memset(w0_s[:].rearrange("p g n -> p (g n)").bitcast(I32), 0)
+        nc.vector.memset(b_s[:].rearrange("p g n -> p (g n)").bitcast(I32), 0)
+        nc.vector.memset(ones[:], 1.0)
+        nc.vector.memset(warm[:], 0.0)
+        make_identity(nc, ident[:])
+
+        nc.gpsimd.dma_start(out=br_row[0:1, :], in_=br.unsqueeze(0))
+        load_x(0, 1)
+        load_words(wr_c, wr_words)
+        load_x(1, 2)
+        load_x(2, 4)
+        load_scales(nc.scalar, wr_s, wr_scales)
+        load_x(4, 6)
+        load_x(6, 8)
+        load_words(a_c, a_words)
+        load_scales(nc.sync, a_s, a_scales)
+        load_words(w0_c, w0_words, 0)
+        load_words(w0_c, w0_words, 1)
+        load_words(b_c, b_words)
+        load_scales(nc.gpsimd, w0_s, w0_scales)
+        load_scales(nc.gpsimd, b_s, b_scales)
+        nc.scalar.activation(out=warm[:], in_=warm[:], func=ACT.Exp)
+
+        def move(engine, dst, src):
+            if engine == "s":
+                nc.scalar.copy(out=dst, in_=src)
+            else:
+                nc.vector.tensor_copy(out=dst, in_=src)
+
+        def x_split(i):
+            xd[i] = keep.tile([P, D], BF16, name="xd", align_bytes=64)
+            nc.vector.tensor_copy(
+                out=xd[i][:].bitcast(F32).rearrange("r (g u p) -> r g u p", g=2, u=2),
+                in_=xs[i].bitcast(F32).rearrange("r (g p u) -> r g u p", g=2, u=2),
+            )
+
+        def x_turn(i):
+            xt_ps[i] = psum_t.tile([P, 4, P], F32, name="t_ps", tag="t_ps")
+            for g in range(2):
+                for u in range(2):
+                    if i in xd:
+                        words = xd[i][:].bitcast(F32)[:, P * (2 * g + u) : P * (2 * g + u + 1)]
+                    else:
+                        words = xs[i].bitcast(F32)[:, 256 * g + u : 256 * (g + 1) : 2]
+                    nc.tensor.transpose(xt_ps[i][:, 2 * g + u, :], words, ident[:])
+
+        def x_out(i, engine):
+            xg[i] = keep.tile([P, 8 * P], BF16, name="xg", align_bytes=64)
+            dst = xg[i][:].bitcast(F32).rearrange("p (g r u) -> p g r u", g=2, u=2)
+            src = xt_ps[i][:].rearrange("p (g u) r -> p g r u", g=2)
+            move(engine, dst, src)
+
+        def x_quant(i):
+            xc[i] = keep.tile([P, 2 * P], U32, name="xc", align_bytes=64)
+            xp[i] = keep.tile([P, 2 * P], U8, name="xp", align_bytes=64)
+            nc.vector.quantize_mx(out=xc[i][:].bitcast(FP8X4), scales=xp[i][:], in_=xg[i][:])
+
+        def by_x(i, g, out, wc, ws, cols, start, stop):
+            nc.tensor.matmul_mx(
+                out=out,
+                lhsT=xc[i][:, P * g : P * (g + 1)].bitcast(FP8X4),
+                lhsT_scale=xp[i][:, P * g : P * (g + 1)],
+                rhs=wc[:, g, cols].bitcast(FP8X4),
+                rhs_scale=ws[:, g, cols],
+                start=start,
+                stop=stop,
+            )
+
+        def logits(b):
+            lt[b] = psum_y.tile([P, 4, P], F32, name="l_ps", tag="y_ps")
+            for j in range(2):
+                for g in range(2):
+                    by_x(2 * b + j, g, lt[b][:, j, :], wr_c, wr_s, slice(0, E), g == 0, g == 1)
+
+        def soft_a(b):
+            ln[b] = four.tile([P, 2, E], F32, name="ln")
+            mn[b] = four.tile([P, 2], F32, name="mn")
+            nc.vector.scalar_tensor_tensor(
+                out=ln[b][:], in0=lt[b][:, 0:2, :], scalar=-1.0, op0=ALU.mult,
+                in1=br_all[:].unsqueeze(1).to_broadcast([P, 2, E]), op1=ALU.subtract,
+            )
+            nc.vector.tensor_reduce(out=mn[b][:], in_=ln[b][:], axis=AX.X, op=ALU.min)
+
+        def soft_b(b):
+            pe[b] = four.tile([P, 2, E], F32, name="pe")
+            sm[b] = four.tile([P, 2], F32, name="sm")
+            for j in range(2):
+                nc.scalar.activation(
+                    out=pe[b][:, j, :], in_=ln[b][:, j, :], func=ACT.Exp,
+                    bias=mn[b][:, j : j + 1], scale=-1.0, accum_out=sm[b][:, j : j + 1],
+                )
+
+        def soft_c(b):
+            sc = four.tile([P, 2], F32, name="sc")
+            rc[b] = four.tile([P, 2], F32, name="rc")
+            nc.vector.tensor_scalar(out=sc[:], in0=sm[b][:], scalar1=1.0 / E, scalar2=None, op0=ALU.mult)
+            nc.vector.reciprocal(out=rc[b][:], in_=sc[:])
+
+        def down(i):
+            ups[i] = psum_u.tile([P, R], F32, name="u_ps")
+            for g in range(2):
+                by_x(i, g, ups[i][:], a_c, a_s, slice(0, R), g == 0, g == 1)
+
+        def gate(i):
+            b, j = i // 2, i % 2
+            if j == 0:
+                zb[b] = four.tile([P, 2, R], BF16, name="zb", align_bytes=64)
+            src = ups[i][:].rearrange("q (p u e) -> q u p e", u=2, e=2)
+            dst = zb[b][:, j, :].rearrange("q (u p e) -> q u p e", u=2, e=2)
+            for u in range(2):
+                nc.vector.scalar_tensor_tensor(
+                    out=dst[:, u], in0=src[:, u], scalar=rc[b][:, j : j + 1], op0=ALU.mult,
+                    in1=pe[b][:, j, :].unsqueeze(2).to_broadcast([P, E, 2]), op1=ALU.mult,
+                )
+
+        def z_turn(b):
+            zt_ps[b] = psum_t.tile([P, 4, P], F32, name="z_ps", tag="t_ps")
+            words = zb[b][:].rearrange("q j k -> q (j k)").bitcast(F32)
+            for k in range(4):
+                nc.tensor.transpose(zt_ps[b][:, k, :], words[:, P * k : P * (k + 1)], ident[:])
+
+        def z_out(b, engine):
+            zg[b] = four.tile([P, 8 * P], BF16, name="zg", align_bytes=64)
+            move(
+                engine,
+                zg[b][:].bitcast(F32).rearrange("p (j r u) -> p j r u", j=2, u=2),
+                zt_ps[b][:].rearrange("p (j u) r -> p j r u", j=2),
+            )
+
+        def z_quant(b):
+            zc[b] = four.tile([P, 2 * P], U32, name="zc", align_bytes=64)
+            zs[b] = four.tile([P, 2 * P], U8, name="zs", align_bytes=64)
+            nc.vector.quantize_mx(out=zc[b][:].bitcast(FP8X4), scales=zs[b][:], in_=zg[b][:])
+
+        def base(i, h):
+            if h == 0:
+                yo[i] = keep.tile([P, F], F32, name="yo")
+                yb[i] = keep.tile([P, F], BF16, name="yb", align_bytes=64)
+            yps[i, h] = psum_y.tile([P, 512], F32, name="y_ps", tag="y_ps")
+            for g in range(2):
+                by_x(i, g, yps[i, h][:], w0_c, w0_s, slice(512 * h, 512 * (h + 1)), g == 0, False)
+
+        def up(i, h):
+            cols = slice(512 * h, 512 * (h + 1))
+            nc.tensor.matmul_mx(
+                out=yps[i, h][:],
+                lhsT=zc[i // 2][:, P * (i % 2) : P * (i % 2 + 1)].bitcast(FP8X4),
+                lhsT_scale=zs[i // 2][:, P * (i % 2) : P * (i % 2 + 1)],
+                rhs=b_c[:, 0, cols].bitcast(FP8X4), rhs_scale=b_s[:, 0, cols],
+                start=False, stop=True,
+            )
+
+        def y_out(i, h, engine):
+            move(engine, yo[i][:, 512 * h : 512 * (h + 1)], yps[i, h][:])
+
+        def y_store(i, h=None):
+            cols = slice(0, F) if h is None else slice(512 * h, 512 * (h + 1))
+            nc.sync.dma_start(out=out_0[P * i : P * (i + 1), cols], in_=yo[i][:, cols])
+
+        def y_round(i, h):
+            cols = slice(512 * h, 512 * (h + 1))
+            nc.vector.tensor_copy(
+                out=yb[i][:, cols].rearrange("q (u p e) -> q u p e", u=2, e=2),
+                in_=yo[i][:, cols].rearrange("q (p u e) -> q u p e", u=2, e=2),
+            )
+
+        def y_turn(i):
+            yt_ps[i] = psum_t.tile([P, 4, P], F32, name="yt_ps", tag="t_ps")
+            words = yb[i][:].bitcast(F32)
+            for k in range(4):
+                nc.tensor.transpose(yt_ps[i][:, k, :], words[:, P * k : P * (k + 1)], ident[:])
+
+        def yt_out(i, engine):
+            yg[i] = keep.tile([P, 8 * P], BF16, name="yg", align_bytes=64)
+            move(
+                engine,
+                yg[i][:].bitcast(F32).rearrange("p (h r u) -> p h r u", h=2, u=2),
+                yt_ps[i][:].rearrange("p (h u) r -> p h r u", h=2),
+            )
+
+        def plane(i):
+            return y_s if i < 6 else y_s2
+
+        def y_quant(i):
+            yc[i] = keep.tile([P, 2, P], U32, name="yc", align_bytes=64)
+            for h in range(2):
+                nc.vector.quantize_mx(
+                    out=yc[i][:, h, :].bitcast(FP8X4),
+                    scales=plane(i)[:, h, P * (i % 6) : P * (i % 6 + 1)],
+                    in_=yg[i][:, 512 * h : 512 * (h + 1)],
+                )
+
+        def words_store(i):
+            nc.sync.dma_start(
+                out=out_1[:, :, P * i : P * (i + 1), :].rearrange("h p r t -> p h (r t)").bitcast(I32),
+                in_=yc[i][:].bitcast(I32),
+            )
+
+        def scales_store(lo, hi, queues):
+            for q in range(4):
+                (nc.scalar if queues[q] == "s" else nc.sync).dma_start(
+                    out=out_2[:, 4 * q : 4 * q + 4, P * lo : P * hi].rearrange("h r n -> r h n").bitcast(I32),
+                    in_=plane(lo)[32 * q : 32 * q + 4].bitcast(I32),
+                )
+
+        def y_round_ps(i, h):
+            nc.vector.tensor_copy(
+                out=yb[i][:, 512 * h : 512 * (h + 1)].rearrange("q (u p e) -> q u p e", u=2, e=2),
+                in_=yps[i, h][:].rearrange("q (p u e) -> q u p e", u=2, e=2),
+            )
+
+        def half_turn(i, h):
+            yt_ps[i, h] = psum_t.tile([P, 4, P], F32, name="yt_ps", tag="t_ps")
+            words = yb[i][:].bitcast(F32)
+            for u in range(2):
+                k = 2 * h + u
+                nc.tensor.transpose(yt_ps[i, h][:, u, :], words[:, P * k : P * (k + 1)], ident[:])
+
+        def half_out(i, h, engine):
+            yg[i, h] = keep.tile([P, 4 * P], BF16, name="ygh", align_bytes=64)
+            move(
+                engine,
+                yg[i, h][:].bitcast(F32).rearrange("p (r u) -> p r u", u=2),
+                yt_ps[i, h][:, 0:2, :].rearrange("p u r -> p r u"),
+            )
+
+        def half_quant(i, h):
+            yc[i, h] = keep.tile([P, P], U32, name="ych", align_bytes=64)
+            nc.vector.quantize_mx(
+                out=yc[i, h][:].bitcast(FP8X4), scales=plane(i)[:, h, P * (i % 6) : P * (i % 6 + 1)], in_=yg[i, h][:]
+            )
+
+        def half_store(i, h):
+            nc.sync.dma_start(
+                out=out_1[h, :, P * i : P * (i + 1), :].rearrange("p r t -> p (r t)").bitcast(I32),
+                in_=yc[i, h][:].bitcast(I32),
+            )
+
+        def half_y_store(i, h):
+            cols = slice(512 * h, 512 * (h + 1))
+            nc.sync.dma_start(out=out_0[P * i : P * (i + 1), cols], in_=yo[i][:, cols])
+
+        def bias():
+            lt["br"] = psum_y.tile([P, 4, P], F32, name="br_ps", tag="y_ps")
+            nc.tensor.matmul(out=lt["br"][:, 0, :], lhsT=ones[:], rhs=br_row[:], start=True, stop=True)
+
+        def bias_out():
+            nc.vector.tensor_copy(out=br_all[:], in_=lt["br"][:, 0, :])
+
+        x_turn(0)
+        x_out(0, "s")
+        x_quant(0)
+        x_turn(1)
+        bias()
+        x_split(2)
+        x_out(1, "s")
+        x_quant(1)
+        logits(0)
+        bias_out()
+        x_turn(2)
+        x_split(3)
+        soft_a(0)
+        x_split(4)
+        x_out(2, "s")
+        x_turn(3)
+        x_turn(4)
+        x_split(5)
+        x_split(6)
+        x_out(3, "s")
+        x_turn(5)
+        x_split(7)
+        x_turn(6)
+        x_out(4, "s")
+        x_turn(7)
+        x_quant(2)
+        x_quant(3)
+        down(0)
+        down(1)
+        soft_b(0)
+        soft_c(0)
+        logits(1)
+        x_out(5, "s")
+        gate(0)
+        down(2)
+        gate(1)
+        x_out(6, "s")
+        x_quant(4)
+        z_turn(0)
+        soft_a(1)
+        x_out(7, "s")
+        z_out(0, "s")
+        soft_b(1)
+        base(0, 0)
+        x_quant(5)
+        down(3)
+        base(0, 1)
+        z_quant(0)
+        up(0, 0)
+        up(0, 1)
+        base(1, 0)
+        up(1, 0)
+        y_out(0, 0, "s")
+        soft_c(1)
+        logits(2)
+        gate(2)
+        gate(3)
+        down(4)
+        y_out(0, 1, "s")
+        base(1, 1)
+        y_round(0, 0)
+        down(5)
+        soft_a(2)
+        up(1, 1)
+        x_quant(6)
+        y_out(1, 0, "s")
+        y_round(0, 1)
+        x_quant(7)
+        y_round(1, 0)
+        soft_b(2)
+        z_turn(1)
+        y_out(1, 1, "s")
+        y_turn(0)
+        z_out(1, "s")
+        soft_c(2)
+        logits(3)
+        gate(4)
+        z_quant(1)
+        base(2, 0)
+        base(2, 1)
+        gate(5)
+        up(2, 0)
+        yt_out(0, "s")
+        down(6)
+        y_round(1, 1)
+        soft_a(3)
+        z_turn(2)
+        y_turn(1)
+        y_out(2, 0, "v")
+        soft_b(3)
+        up(2, 1)
+        z_out(2, "v")
+        y_quant(0)
+        base(3, 0)
+        z_quant(2)
+        up(3, 0)
+        y_round(2, 0)
+        yt_out(1, "s")
+        y_out(2, 1, "s")
+        base(3, 1)
+        up(3, 1)
+        down(7)
+        soft_c(3)
+        y_round(2, 1)
+        gate(6)
+        y_out(3, 0, "s")
+        gate(7)
+        y_out(3, 1, "s")
+        base(4, 0)
+        y_store(0)
+        y_round(3, 0)
+        up(4, 0)
+        y_out(4, 0, "s")
+        y_round(3, 1)
+        base(4, 1)
+        y_store(1)
+        up(4, 1)
+        y_out(4, 1, "s")
+        z_turn(3)
+        y_round(4, 0)
+        words_store(0)
+        y_turn(2)
+        y_turn(3)
+        z_out(3, "s")
+        base(5, 0)
+        up(5, 0)
+        y_quant(1)
+        base(5, 1)
+        up(5, 1)
+        yt_out(2, "s")
+        y_out(5, 0, "s")
+        y_store(2)
+        yt_out(3, "v")
+        y_store(3)
+        z_quant(3)
+        base(6, 0)
+        y_out(5, 1, "s")
+        y_quant(2)
+        y_round(4, 1)
+        y_quant(3)
+        base(6, 1)
+        up(6, 0)
+        up(6, 1)
+        words_store(1)
+        y_round(5, 0)
+        y_store(4)
+        y_turn(4)
+        y_round(5, 1)
+        y_out(6, 0, "v")
+        y_turn(5)
+        y_out(6, 1, "s")
+        yt_out(4, "s")
+        words_store(2)
+        y_round(6, 0)
+        base(7, 0)
+        yt_out(5, "v")
+        up(7, 0)
+        y_quant(4)
+        y_quant(5)
+        base(7, 1)
+        up(7, 1)
+        words_store(3)
+        y_out(7, 0, "s")
+        y_round(6, 1)
+        y_turn(6)
+        y_store(5)
+        y_out(7, 1, "s")
+        y_round(7, 0)
+        yt_out(6, "s")
+        y_store(6)
+        y_round_ps(7, 1)
+        half_turn(7, 0)
+        half_out(7, 0, "v")
+        words_store(4)
+        words_store(5)
+        half_quant(7, 0)
+        half_turn(7, 1)
+        half_y_store(7, 0)
+        scales_store(0, 6, "yyyy")
+        half_out(7, 1, "s")
+        y_quant(6)
+        half_y_store(7, 1)
+        half_store(7, 0)
+        half_quant(7, 1)
+        words_store(6)
+        scales_store(6, 8, "sysy")
+        half_store(7, 1)

@@ -47,8 +47,8 @@ def tile_rankwisemoloradenserouter_x2_kernel(
         a_s = const.tile([P, 2, R], U8, name="a_s", align_bytes=64)
         b_c = const.tile([P, 1, F], U32, name="b_c", align_bytes=64)
         b_s = const.tile([P, 1, F], U8, name="b_s", align_bytes=64)
-        y_s = const.tile([P, 2, 6 * P], U8, name="y_s", align_bytes=64)
-        y_s2 = const.tile([P, 2, 2 * P], U8, name="y_s2", align_bytes=64)
+        y_s = const.tile([P, 2, 4 * P], U8, name="y_s", align_bytes=64)
+        y_s2 = const.tile([P, 2, 4 * P], U8, name="y_s2", align_bytes=64)
 
         xs, xd, xg, xc, xp, xt_ps = {}, {}, {}, {}, {}, {}
         lt, ln, mn, sm, pe, rc = {}, {}, {}, {}, {}, {}
@@ -88,15 +88,15 @@ def tile_rankwisemoloradenserouter_x2_kernel(
         make_identity(nc, ident[:])
 
         nc.gpsimd.dma_start(out=br_row[0:1, :], in_=br.unsqueeze(0))
+        load_scales(nc.scalar, wr_s, wr_scales)
         load_x(0, 1)
         load_words(wr_c, wr_words)
         load_x(1, 2)
         load_x(2, 4)
-        load_scales(nc.scalar, wr_s, wr_scales)
+        load_scales(nc.sync, a_s, a_scales)
         load_x(4, 6)
         load_x(6, 8)
         load_words(a_c, a_words)
-        load_scales(nc.sync, a_s, a_scales)
         load_words(w0_c, w0_words, 0)
         load_words(w0_c, w0_words, 1)
         load_words(b_c, b_words)
@@ -262,14 +262,14 @@ def tile_rankwisemoloradenserouter_x2_kernel(
             )
 
         def plane(i):
-            return y_s if i < 6 else y_s2
+            return y_s if i < 4 else y_s2
 
         def y_quant(i):
             yc[i] = keep.tile([P, 2, P], U32, name="yc", align_bytes=64)
             for h in range(2):
                 nc.vector.quantize_mx(
                     out=yc[i][:, h, :].bitcast(FP8X4),
-                    scales=plane(i)[:, h, P * (i % 6) : P * (i % 6 + 1)],
+                    scales=plane(i)[:, h, P * (i % 4) : P * (i % 4 + 1)],
                     in_=yg[i][:, 512 * h : 512 * (h + 1)],
                 )
 
@@ -281,7 +281,7 @@ def tile_rankwisemoloradenserouter_x2_kernel(
 
         def scales_store(lo, hi, queues):
             for q in range(4):
-                (nc.scalar if queues[q] == "s" else nc.sync).dma_start(
+                {"s": nc.scalar, "y": nc.sync, "p": nc.gpsimd}[queues[q]].dma_start(
                     out=out_2[:, 4 * q : 4 * q + 4, P * lo : P * hi].rearrange("h r n -> r h n").bitcast(I32),
                     in_=plane(lo)[32 * q : 32 * q + 4].bitcast(I32),
                 )
@@ -310,7 +310,7 @@ def tile_rankwisemoloradenserouter_x2_kernel(
         def half_quant(i, h):
             yc[i, h] = keep.tile([P, P], U32, name="ych", align_bytes=64)
             nc.vector.quantize_mx(
-                out=yc[i, h][:].bitcast(FP8X4), scales=plane(i)[:, h, P * (i % 6) : P * (i % 6 + 1)], in_=yg[i, h][:]
+                out=yc[i, h][:].bitcast(FP8X4), scales=plane(i)[:, h, P * (i % 4) : P * (i % 4 + 1)], in_=yg[i, h][:]
             )
 
         def half_store(i, h):
@@ -331,189 +331,189 @@ def tile_rankwisemoloradenserouter_x2_kernel(
             nc.vector.tensor_copy(out=br_all[:], in_=lt["br"][:, 0, :])
 
         x_turn(0)
-        x_out(0, "s")
-        x_quant(0)
+        x_split(2)
         x_turn(1)
         bias()
-        x_split(2)
+        x_turn(2)
+        x_out(0, "s")
+        bias_out()
+        x_split(3)
+        x_quant(0)
         x_out(1, "s")
         x_quant(1)
-        logits(0)
-        bias_out()
-        x_turn(2)
-        x_split(3)
-        soft_a(0)
         x_split(4)
         x_out(2, "s")
         x_turn(3)
-        x_turn(4)
-        x_split(5)
-        x_split(6)
         x_out(3, "s")
+        x_split(5)
+        logits(0)
+        soft_a(0)
+        x_split(6)
+        x_turn(4)
         x_turn(5)
         x_split(7)
         x_turn(6)
         x_out(4, "s")
-        x_turn(7)
+        soft_b(0)
         x_quant(2)
         x_quant(3)
+        soft_c(0)
+        x_turn(7)
         down(0)
         down(1)
-        soft_b(0)
-        soft_c(0)
+        x_quant(4)
         logits(1)
         x_out(5, "s")
-        gate(0)
-        down(2)
-        gate(1)
-        x_out(6, "s")
-        x_quant(4)
-        z_turn(0)
-        soft_a(1)
-        x_out(7, "s")
-        z_out(0, "s")
-        soft_b(1)
         base(0, 0)
+        gate(0)
+        x_out(6, "s")
+        gate(1)
+        z_turn(0)
+        z_out(0, "s")
+        soft_a(1)
+        down(2)
         x_quant(5)
-        down(3)
         base(0, 1)
+        soft_b(1)
         z_quant(0)
+        logits(2)
         up(0, 0)
+        soft_c(1)
+        down(3)
+        soft_a(2)
+        x_out(7, "s")
+        gate(2)
+        y_out(0, 0, "s")
         up(0, 1)
         base(1, 0)
-        up(1, 0)
-        y_out(0, 0, "s")
-        soft_c(1)
-        logits(2)
-        gate(2)
-        gate(3)
-        down(4)
         y_out(0, 1, "s")
-        base(1, 1)
+        soft_b(2)
+        gate(3)
+        y_store(0)
         y_round(0, 0)
-        down(5)
-        soft_a(2)
+        y_round(0, 1)
+        up(1, 0)
+        y_out(1, 0, "s")
+        y_round(1, 0)
+        base(1, 1)
         up(1, 1)
         x_quant(6)
-        y_out(1, 0, "s")
-        y_round(0, 1)
-        x_quant(7)
-        y_round(1, 0)
-        soft_b(2)
         z_turn(1)
+        x_quant(7)
         y_out(1, 1, "s")
-        y_turn(0)
+        down(4)
+        base(2, 0)
         z_out(1, "s")
+        z_quant(1)
+        down(5)
+        up(2, 0)
+        y_out(2, 0, "s")
         soft_c(2)
         logits(3)
-        gate(4)
-        z_quant(1)
-        base(2, 0)
         base(2, 1)
-        gate(5)
-        up(2, 0)
-        yt_out(0, "s")
-        down(6)
-        y_round(1, 1)
-        soft_a(3)
-        z_turn(2)
-        y_turn(1)
-        y_out(2, 0, "v")
-        soft_b(3)
         up(2, 1)
-        z_out(2, "v")
-        y_quant(0)
+        y_round(1, 1)
         base(3, 0)
-        z_quant(2)
         up(3, 0)
-        y_round(2, 0)
-        yt_out(1, "s")
+        y_turn(0)
+        gate(4)
         y_out(2, 1, "s")
+        y_round(2, 0)
+        yt_out(0, "s")
+        y_turn(1)
+        gate(5)
+        z_turn(2)
+        soft_a(3)
+        down(6)
+        z_out(2, "s")
         base(3, 1)
-        up(3, 1)
-        down(7)
-        soft_c(3)
-        y_round(2, 1)
-        gate(6)
-        y_out(3, 0, "s")
-        gate(7)
-        y_out(3, 1, "s")
+        yt_out(1, "v")
         base(4, 0)
-        y_store(0)
+        down(7)
+        y_quant(0)
+        y_out(3, 0, "v")
+        up(3, 1)
+        soft_b(3)
+        z_quant(2)
+        y_round(2, 1)
         y_round(3, 0)
         up(4, 0)
-        y_out(4, 0, "s")
-        y_round(3, 1)
-        base(4, 1)
         y_store(1)
+        y_out(3, 1, "s")
+        soft_c(3)
+        base(4, 1)
         up(4, 1)
-        y_out(4, 1, "s")
-        z_turn(3)
-        y_round(4, 0)
-        words_store(0)
-        y_turn(2)
-        y_turn(3)
-        z_out(3, "s")
         base(5, 0)
         up(5, 0)
-        y_quant(1)
-        base(5, 1)
-        up(5, 1)
-        yt_out(2, "s")
-        y_out(5, 0, "s")
+        y_out(4, 0, "s")
+        y_out(4, 1, "s")
+        gate(6)
+        gate(7)
+        y_turn(2)
+        z_turn(3)
         y_store(2)
-        yt_out(3, "v")
+        y_round(3, 1)
+        y_turn(3)
+        y_quant(1)
+        yt_out(2, "s")
+        yt_out(3, "s")
+        base(5, 1)
+        words_store(0)
         y_store(3)
-        z_quant(3)
-        base(6, 0)
-        y_out(5, 1, "s")
+        z_out(3, "v")
+        up(5, 1)
         y_quant(2)
-        y_round(4, 1)
+        y_out(5, 0, "s")
+        z_quant(3)
         y_quant(3)
-        base(6, 1)
+        y_round(4, 0)
+        base(6, 0)
+        y_round(4, 1)
         up(6, 0)
-        up(6, 1)
+        base(6, 1)
         words_store(1)
-        y_round(5, 0)
-        y_store(4)
+        scales_store(0, 4, "pppp")
+        y_out(5, 1, "s")
+        up(6, 1)
+        y_out(6, 0, "s")
         y_turn(4)
+        base(7, 0)
+        up(7, 0)
+        base(7, 1)
+        y_round(5, 0)
         y_round(5, 1)
-        y_out(6, 0, "v")
-        y_turn(5)
         y_out(6, 1, "s")
+        y_round(6, 0)
+        y_store(4)
+        y_round(6, 1)
         yt_out(4, "s")
         words_store(2)
-        y_round(6, 0)
-        base(7, 0)
-        yt_out(5, "v")
-        up(7, 0)
-        y_quant(4)
-        y_quant(5)
-        base(7, 1)
-        up(7, 1)
         words_store(3)
-        y_out(7, 0, "s")
-        y_round(6, 1)
-        y_turn(6)
         y_store(5)
-        y_out(7, 1, "s")
+        up(7, 1)
+        y_turn(5)
+        y_quant(4)
+        y_out(7, 0, "s")
         y_round(7, 0)
-        yt_out(6, "s")
-        y_store(6)
         y_round_ps(7, 1)
+        y_out(7, 1, "s")
+        yt_out(5, "s")
+        y_turn(6)
         half_turn(7, 0)
-        half_out(7, 0, "v")
-        words_store(4)
-        words_store(5)
-        half_quant(7, 0)
+        yt_out(6, "v")
+        y_quant(5)
         half_turn(7, 1)
-        half_y_store(7, 0)
-        scales_store(0, 6, "yyyy")
+        half_out(7, 0, "s")
         half_out(7, 1, "s")
+        y_store(6)
+        half_quant(7, 0)
+        words_store(4)
+        half_y_store(7, 0)
         y_quant(6)
-        half_y_store(7, 1)
-        half_store(7, 0)
         half_quant(7, 1)
+        half_y_store(7, 1)
+        scales_store(4, 8, "sysy")
+        words_store(5)
         words_store(6)
-        scales_store(6, 8, "sysy")
+        half_store(7, 0)
         half_store(7, 1)

@@ -88,20 +88,20 @@ def tile_rankwisemoloradenserouter_x2_kernel(
         make_identity(nc, ident[:])
 
         nc.gpsimd.dma_start(out=br_row[0:1, :], in_=br.unsqueeze(0))
-        load_scales(nc.scalar, wr_s, wr_scales)
         load_x(0, 1)
         load_words(wr_c, wr_words)
         load_x(1, 2)
         load_x(2, 4)
-        load_scales(nc.sync, a_s, a_scales)
+        load_scales(nc.scalar, wr_s, wr_scales)
         load_x(4, 6)
         load_x(6, 8)
         load_words(a_c, a_words)
         load_words(w0_c, w0_words, 0)
         load_words(w0_c, w0_words, 1)
         load_words(b_c, b_words)
+        load_scales(nc.sync, b_s, b_scales)
+        load_scales(nc.gpsimd, a_s, a_scales)
         load_scales(nc.gpsimd, w0_s, w0_scales)
-        load_scales(nc.gpsimd, b_s, b_scales)
         nc.scalar.activation(out=warm[:], in_=warm[:], func=ACT.Exp)
 
         def move(engine, dst, src):
@@ -265,18 +265,23 @@ def tile_rankwisemoloradenserouter_x2_kernel(
             return y_s if i < 4 else y_s2
 
         def y_quant(i):
-            yc[i] = keep.tile([P, 2, P], U32, name="yc", align_bytes=64)
             for h in range(2):
-                nc.vector.quantize_mx(
-                    out=yc[i][:, h, :].bitcast(FP8X4),
-                    scales=plane(i)[:, h, P * (i % 4) : P * (i % 4 + 1)],
-                    in_=yg[i][:, 512 * h : 512 * (h + 1)],
-                )
+                quantize_half(i, h, yg[i][:, 512 * h : 512 * (h + 1)])
 
-        def words_store(i):
+        def quantize_half(i, h, values):
+            b = i // 2
+            if b not in yc:
+                yc[b] = four.tile([P, 2, 2 * P], U32, name="yc", align_bytes=64)
+            nc.vector.quantize_mx(
+                out=yc[b][:, h, P * (i % 2) : P * (i % 2 + 1)].bitcast(FP8X4),
+                scales=plane(i)[:, h, P * (i % 4) : P * (i % 4 + 1)],
+                in_=values,
+            )
+
+        def words_store(lo, hi):
             nc.sync.dma_start(
-                out=out_1[:, :, P * i : P * (i + 1), :].rearrange("h p r t -> p h (r t)").bitcast(I32),
-                in_=yc[i][:].bitcast(I32),
+                out=out_1[:, :, P * lo : P * hi, :].rearrange("h p r t -> p h (r t)").bitcast(I32),
+                in_=yc[lo // 2][:, :, P * (lo % 2) : P * (lo % 2) + P * (hi - lo)].bitcast(I32),
             )
 
         def scales_store(lo, hi, queues):
@@ -308,16 +313,7 @@ def tile_rankwisemoloradenserouter_x2_kernel(
             )
 
         def half_quant(i, h):
-            yc[i, h] = keep.tile([P, P], U32, name="ych", align_bytes=64)
-            nc.vector.quantize_mx(
-                out=yc[i, h][:].bitcast(FP8X4), scales=plane(i)[:, h, P * (i % 4) : P * (i % 4 + 1)], in_=yg[i, h][:]
-            )
-
-        def half_store(i, h):
-            nc.sync.dma_start(
-                out=out_1[h, :, P * i : P * (i + 1), :].rearrange("p r t -> p (r t)").bitcast(I32),
-                in_=yc[i, h][:].bitcast(I32),
-            )
+            quantize_half(i, h, yg[i, h][:])
 
         def half_y_store(i, h):
             cols = slice(512 * h, 512 * (h + 1))
@@ -331,189 +327,185 @@ def tile_rankwisemoloradenserouter_x2_kernel(
             nc.vector.tensor_copy(out=br_all[:], in_=lt["br"][:, 0, :])
 
         x_turn(0)
-        x_split(2)
         x_turn(1)
+        x_out(0, "v")
         bias()
-        x_turn(2)
-        x_out(0, "s")
-        bias_out()
-        x_split(3)
         x_quant(0)
+        x_split(2)
         x_out(1, "s")
+        x_split(3)
         x_quant(1)
-        x_split(4)
-        x_out(2, "s")
-        x_turn(3)
-        x_out(3, "s")
-        x_split(5)
+        x_turn(2)
         logits(0)
+        bias_out()
+        x_turn(3)
+        x_out(2, "s")
+        x_split(4)
+        x_split(5)
         soft_a(0)
-        x_split(6)
         x_turn(4)
         x_turn(5)
-        x_split(7)
-        x_turn(6)
-        x_out(4, "s")
+        x_out(3, "s")
         soft_b(0)
+        x_split(6)
+        x_out(4, "s")
         x_quant(2)
         x_quant(3)
-        soft_c(0)
-        x_turn(7)
-        down(0)
-        down(1)
-        x_quant(4)
+        x_split(7)
+        x_turn(6)
         logits(1)
-        x_out(5, "s")
-        base(0, 0)
+        soft_c(0)
+        down(0)
+        soft_a(1)
         gate(0)
-        x_out(6, "s")
+        x_turn(7)
+        down(1)
+        x_out(5, "s")
+        down(2)
         gate(1)
         z_turn(0)
-        z_out(0, "s")
-        soft_a(1)
-        down(2)
-        x_quant(5)
-        base(0, 1)
         soft_b(1)
-        z_quant(0)
-        logits(2)
-        up(0, 0)
         soft_c(1)
         down(3)
-        soft_a(2)
+        x_quant(4)
+        x_quant(5)
+        x_out(6, "s")
         x_out(7, "s")
+        z_out(0, "s")
+        base(0, 0)
+        base(0, 1)
+        z_quant(0)
+        up(0, 0)
         gate(2)
-        y_out(0, 0, "s")
+        logits(2)
         up(0, 1)
+        gate(3)
+        soft_a(2)
+        y_out(0, 0, "s")
+        z_turn(1)
         base(1, 0)
         y_out(0, 1, "s")
-        soft_b(2)
-        gate(3)
-        y_store(0)
-        y_round(0, 0)
-        y_round(0, 1)
-        up(1, 0)
-        y_out(1, 0, "s")
-        y_round(1, 0)
-        base(1, 1)
-        up(1, 1)
-        x_quant(6)
-        z_turn(1)
-        x_quant(7)
-        y_out(1, 1, "s")
         down(4)
-        base(2, 0)
+        y_round(0, 0)
+        soft_b(2)
         z_out(1, "s")
-        z_quant(1)
-        down(5)
-        up(2, 0)
-        y_out(2, 0, "s")
+        up(1, 0)
+        y_round(0, 1)
+        x_quant(6)
+        x_quant(7)
         soft_c(2)
+        base(1, 1)
+        base(2, 0)
+        up(1, 1)
+        z_quant(1)
+        y_out(1, 0, "v")
+        down(5)
+        gate(4)
+        y_store(0)
         logits(3)
+        y_out(1, 1, "s")
+        up(2, 0)
+        down(6)
         base(2, 1)
         up(2, 1)
+        y_round(1, 0)
         y_round(1, 1)
+        soft_a(3)
+        y_out(2, 0, "s")
+        y_out(2, 1, "s")
+        gate(5)
+        y_store(1)
+        y_turn(0)
+        y_round(2, 0)
+        yt_out(0, "v")
+        y_turn(1)
+        soft_b(3)
+        y_round(2, 1)
+        z_turn(2)
         base(3, 0)
         up(3, 0)
-        y_turn(0)
-        gate(4)
-        y_out(2, 1, "s")
-        y_round(2, 0)
-        yt_out(0, "s")
-        y_turn(1)
-        gate(5)
-        z_turn(2)
-        soft_a(3)
-        down(6)
         z_out(2, "s")
-        base(3, 1)
-        yt_out(1, "v")
-        base(4, 0)
-        down(7)
-        y_quant(0)
-        y_out(3, 0, "v")
-        up(3, 1)
-        soft_b(3)
         z_quant(2)
-        y_round(2, 1)
-        y_round(3, 0)
-        up(4, 0)
-        y_store(1)
-        y_out(3, 1, "s")
+        base(3, 1)
+        up(3, 1)
+        base(4, 0)
         soft_c(3)
-        base(4, 1)
-        up(4, 1)
-        base(5, 0)
-        up(5, 0)
-        y_out(4, 0, "s")
-        y_out(4, 1, "s")
+        y_out(3, 0, "s")
         gate(6)
-        gate(7)
-        y_turn(2)
-        z_turn(3)
-        y_store(2)
+        up(4, 0)
+        down(7)
+        base(4, 1)
+        y_round(3, 0)
+        y_out(3, 1, "s")
+        y_out(4, 0, "s")
+        y_quant(0)
+        up(4, 1)
+        yt_out(1, "s")
+        y_out(4, 1, "s")
         y_round(3, 1)
-        y_turn(3)
+        y_store(2)
+        gate(7)
         y_quant(1)
-        yt_out(2, "s")
-        yt_out(3, "s")
-        base(5, 1)
-        words_store(0)
-        y_store(3)
-        z_out(3, "v")
-        up(5, 1)
-        y_quant(2)
-        y_out(5, 0, "s")
-        z_quant(3)
-        y_quant(3)
+        base(5, 0)
+        z_turn(3)
         y_round(4, 0)
+        y_turn(2)
+        z_out(3, "v")
+        y_turn(3)
+        z_quant(3)
+        up(5, 0)
+        base(5, 1)
+        yt_out(2, "v")
+        y_quant(2)
+        y_store(3)
+        words_store(0, 2)
+        up(5, 1)
+        yt_out(3, "s")
+        y_quant(3)
         base(6, 0)
-        y_round(4, 1)
+        y_out(5, 0, "s")
         up(6, 0)
+        y_round(4, 1)
+        y_round(5, 0)
+        y_store(4)
         base(6, 1)
-        words_store(1)
-        scales_store(0, 4, "pppp")
         y_out(5, 1, "s")
-        up(6, 1)
         y_out(6, 0, "s")
-        y_turn(4)
+        up(6, 1)
+        y_store(5)
         base(7, 0)
         up(7, 0)
-        base(7, 1)
-        y_round(5, 0)
         y_round(5, 1)
-        y_out(6, 1, "s")
-        y_round(6, 0)
-        y_store(4)
-        y_round(6, 1)
-        yt_out(4, "s")
-        words_store(2)
-        words_store(3)
-        y_store(5)
-        up(7, 1)
+        y_turn(4)
         y_turn(5)
-        y_quant(4)
-        y_out(7, 0, "s")
+        words_store(2, 4)
+        y_round(6, 0)
+        y_out(6, 1, "s")
+        y_out(7, 0, "v")
+        y_round(6, 1)
+        scales_store(0, 4, "yyyy")
+        base(7, 1)
+        yt_out(4, "s")
         y_round(7, 0)
-        y_round_ps(7, 1)
-        y_out(7, 1, "s")
+        up(7, 1)
+        half_turn(7, 0)
+        y_quant(4)
         yt_out(5, "s")
         y_turn(6)
-        half_turn(7, 0)
-        yt_out(6, "v")
-        y_quant(5)
-        half_turn(7, 1)
-        half_out(7, 0, "s")
-        half_out(7, 1, "s")
+        y_round_ps(7, 1)
         y_store(6)
-        half_quant(7, 0)
-        words_store(4)
+        half_out(7, 0, "s")
+        y_quant(5)
+        yt_out(6, "s")
         half_y_store(7, 0)
+        half_quant(7, 0)
+        half_turn(7, 1)
+        half_out(7, 1, "s")
         y_quant(6)
         half_quant(7, 1)
-        half_y_store(7, 1)
+        words_store(4, 6)
+        y_out(7, 1, "s")
+        words_store(6, 7)
         scales_store(4, 8, "sysy")
-        words_store(5)
-        words_store(6)
-        half_store(7, 0)
-        half_store(7, 1)
+        half_y_store(7, 1)
+        words_store(7, 8)

@@ -90,18 +90,17 @@ def tile_rankwisemoloradenserouter_x2_kernel(
         nc.gpsimd.dma_start(out=br_row[0:1, :], in_=br.unsqueeze(0))
         load_x(0, 1)
         load_words(wr_c, wr_words)
-        load_x(1, 2)
-        load_x(2, 4)
-        load_scales(nc.scalar, wr_s, wr_scales)
+        load_scales(nc.sync, wr_s, wr_scales)
+        load_x(1, 4)
         load_x(4, 6)
         load_x(6, 8)
         load_words(a_c, a_words)
+        load_scales(nc.sync, a_s, a_scales)
         load_words(w0_c, w0_words, 0)
         load_words(w0_c, w0_words, 1)
+        load_scales(nc.sync, w0_s, w0_scales)
         load_words(b_c, b_words)
         load_scales(nc.sync, b_s, b_scales)
-        load_scales(nc.gpsimd, a_s, a_scales)
-        load_scales(nc.gpsimd, w0_s, w0_scales)
         nc.scalar.activation(out=warm[:], in_=warm[:], func=ACT.Exp)
 
         def move(engine, dst, src):
@@ -269,11 +268,11 @@ def tile_rankwisemoloradenserouter_x2_kernel(
                 quantize_half(i, h, yg[i][:, 512 * h : 512 * (h + 1)])
 
         def quantize_half(i, h, values):
-            b = i // 2
-            if b not in yc:
-                yc[b] = four.tile([P, 2, 2 * P], U32, name="yc", align_bytes=64)
+            first = i if i >= 6 else i - i % 2
+            if first not in yc:
+                yc[first] = four.tile([P, 2, P if i >= 6 else 2 * P], U32, name="yc%d" % (i // 6), align_bytes=64)
             nc.vector.quantize_mx(
-                out=yc[b][:, h, P * (i % 2) : P * (i % 2 + 1)].bitcast(FP8X4),
+                out=yc[first][:, h, P * (i - first) : P * (i - first + 1)].bitcast(FP8X4),
                 scales=plane(i)[:, h, P * (i % 4) : P * (i % 4 + 1)],
                 in_=values,
             )
@@ -281,7 +280,7 @@ def tile_rankwisemoloradenserouter_x2_kernel(
         def words_store(lo, hi):
             nc.sync.dma_start(
                 out=out_1[:, :, P * lo : P * hi, :].rearrange("h p r t -> p h (r t)").bitcast(I32),
-                in_=yc[lo // 2][:, :, P * (lo % 2) : P * (lo % 2) + P * (hi - lo)].bitcast(I32),
+                in_=yc[lo][:].bitcast(I32),
             )
 
         def scales_store(lo, hi, queues):
@@ -330,181 +329,181 @@ def tile_rankwisemoloradenserouter_x2_kernel(
         x_turn(1)
         x_out(0, "v")
         bias()
-        x_quant(0)
         x_split(2)
+        x_quant(0)
         x_out(1, "s")
         x_split(3)
-        x_quant(1)
         x_turn(2)
-        logits(0)
+        x_out(2, "s")
         bias_out()
         x_turn(3)
-        x_out(2, "s")
         x_split(4)
         x_split(5)
-        soft_a(0)
-        x_turn(4)
-        x_turn(5)
+        x_quant(1)
         x_out(3, "s")
-        soft_b(0)
-        x_split(6)
-        x_out(4, "s")
+        logits(0)
         x_quant(2)
+        x_split(6)
         x_quant(3)
-        x_split(7)
-        x_turn(6)
+        x_turn(4)
         logits(1)
-        soft_c(0)
+        x_split(7)
+        x_out(4, "s")
+        soft_a(0)
+        x_turn(5)
         down(0)
-        soft_a(1)
-        gate(0)
-        x_turn(7)
+        x_turn(6)
         down(1)
-        x_out(5, "s")
-        down(2)
-        gate(1)
-        z_turn(0)
-        soft_b(1)
-        soft_c(1)
-        down(3)
         x_quant(4)
-        x_quant(5)
+        x_out(5, "s")
+        soft_b(0)
         x_out(6, "s")
-        x_out(7, "s")
+        soft_a(1)
+        soft_c(0)
+        x_quant(5)
+        gate(0)
+        gate(1)
+        x_turn(7)
+        soft_b(1)
+        logits(2)
+        down(2)
+        soft_c(1)
+        gate(2)
+        soft_a(2)
+        z_turn(0)
+        down(3)
         z_out(0, "s")
         base(0, 0)
         base(0, 1)
-        z_quant(0)
-        up(0, 0)
-        gate(2)
-        logits(2)
-        up(0, 1)
         gate(3)
-        soft_a(2)
-        y_out(0, 0, "s")
-        z_turn(1)
+        z_quant(0)
         base(1, 0)
-        y_out(0, 1, "s")
-        down(4)
-        y_round(0, 0)
         soft_b(2)
-        z_out(1, "s")
-        up(1, 0)
-        y_round(0, 1)
+        down(4)
         x_quant(6)
-        x_quant(7)
-        soft_c(2)
-        base(1, 1)
-        base(2, 0)
-        up(1, 1)
-        z_quant(1)
-        y_out(1, 0, "v")
         down(5)
+        x_out(7, "s")
+        soft_c(2)
+        x_quant(7)
+        up(0, 0)
+        up(0, 1)
         gate(4)
-        y_store(0)
+        y_out(0, 0, "s")
+        up(1, 0)
+        y_out(0, 1, "s")
+        z_turn(1)
+        base(1, 1)
+        up(1, 1)
         logits(3)
-        y_out(1, 1, "s")
-        up(2, 0)
+        z_out(1, "v")
+        y_out(1, 0, "s")
+        y_round(0, 0)
         down(6)
-        base(2, 1)
-        up(2, 1)
-        y_round(1, 0)
-        y_round(1, 1)
-        soft_a(3)
-        y_out(2, 0, "s")
-        y_out(2, 1, "s")
         gate(5)
-        y_store(1)
-        y_turn(0)
-        y_round(2, 0)
-        yt_out(0, "v")
-        y_turn(1)
-        soft_b(3)
-        y_round(2, 1)
-        z_turn(2)
+        y_out(1, 1, "s")
+        base(2, 0)
+        base(2, 1)
+        z_quant(1)
+        soft_a(3)
+        y_round(0, 1)
+        up(2, 0)
         base(3, 0)
-        up(3, 0)
-        z_out(2, "s")
-        z_quant(2)
-        base(3, 1)
-        up(3, 1)
-        base(4, 0)
+        y_round(1, 0)
+        y_out(2, 0, "s")
+        y_round(1, 1)
+        y_round(2, 0)
+        y_store(0)
+        soft_b(3)
         soft_c(3)
-        y_out(3, 0, "s")
-        gate(6)
-        up(4, 0)
-        down(7)
-        base(4, 1)
-        y_round(3, 0)
-        y_out(3, 1, "s")
-        y_out(4, 0, "s")
-        y_quant(0)
-        up(4, 1)
+        up(2, 1)
+        y_turn(0)
+        y_turn(1)
+        y_out(2, 1, "s")
+        z_turn(2)
+        yt_out(0, "s")
+        up(3, 0)
+        z_out(2, "v")
+        base(3, 1)
         yt_out(1, "s")
+        down(7)
+        y_out(3, 0, "s")
+        y_round(2, 1)
+        y_quant(0)
+        gate(6)
+        up(3, 1)
+        y_out(3, 1, "s")
+        z_quant(2)
+        base(4, 0)
+        base(4, 1)
+        up(4, 0)
+        y_out(4, 0, "s")
+        up(4, 1)
+        y_round(3, 0)
+        gate(7)
+        z_turn(3)
         y_out(4, 1, "s")
         y_round(3, 1)
-        y_store(2)
-        gate(7)
-        y_quant(1)
-        base(5, 0)
-        z_turn(3)
-        y_round(4, 0)
+        y_store(1)
         y_turn(2)
         z_out(3, "v")
+        y_store(2)
+        y_round(4, 0)
+        yt_out(2, "s")
+        y_quant(1)
         y_turn(3)
-        z_quant(3)
-        up(5, 0)
-        base(5, 1)
-        yt_out(2, "v")
-        y_quant(2)
+        base(5, 0)
         y_store(3)
-        words_store(0, 2)
-        up(5, 1)
+        y_quant(2)
+        y_round(4, 1)
         yt_out(3, "s")
+        y_store(4)
+        up(5, 0)
+        z_quant(3)
+        words_store(0, 2)
+        base(5, 1)
         y_quant(3)
         base(6, 0)
         y_out(5, 0, "s")
-        up(6, 0)
-        y_round(4, 1)
+        up(5, 1)
         y_round(5, 0)
-        y_store(4)
-        base(6, 1)
         y_out(5, 1, "s")
-        y_out(6, 0, "s")
+        up(6, 0)
+        base(6, 1)
         up(6, 1)
-        y_store(5)
+        y_out(6, 0, "v")
+        words_store(2, 4)
+        y_turn(4)
         base(7, 0)
         up(7, 0)
         y_round(5, 1)
-        y_turn(4)
-        y_turn(5)
-        words_store(2, 4)
-        y_round(6, 0)
-        y_out(6, 1, "s")
-        y_out(7, 0, "v")
-        y_round(6, 1)
-        scales_store(0, 4, "yyyy")
-        base(7, 1)
         yt_out(4, "s")
-        y_round(7, 0)
+        y_out(6, 1, "v")
+        y_round(6, 0)
+        base(7, 1)
+        scales_store(0, 4, "yyyy")
         up(7, 1)
-        half_turn(7, 0)
-        y_quant(4)
-        yt_out(5, "s")
+        y_turn(5)
+        y_out(7, 0, "s")
+        y_round(6, 1)
+        y_store(5)
         y_turn(6)
-        y_round_ps(7, 1)
+        y_quant(4)
+        y_round(7, 0)
         y_store(6)
-        half_out(7, 0, "s")
-        y_quant(5)
-        yt_out(6, "s")
+        y_round_ps(7, 1)
+        half_turn(7, 0)
         half_y_store(7, 0)
-        half_quant(7, 0)
+        yt_out(5, "s")
         half_turn(7, 1)
+        half_out(7, 0, "v")
+        yt_out(6, "s")
+        y_quant(5)
         half_out(7, 1, "s")
+        half_quant(7, 0)
+        y_out(7, 1, "s")
+        words_store(4, 6)
         y_quant(6)
         half_quant(7, 1)
-        words_store(4, 6)
-        y_out(7, 1, "s")
         words_store(6, 7)
         scales_store(4, 8, "sysy")
         half_y_store(7, 1)

from contextlib import ExitStack

import concourse.mybir as mybir
from concourse.masks import make_identity

T, D, F, E, R = 1024, 1024, 1024, 128, 512
FLOPS = 2 * T * (D * F + D * E + D * R + R * F)

F32 = mybir.dt.float32
BF16 = mybir.dt.bfloat16
I32 = mybir.dt.int32
U32 = mybir.dt.uint32
U8 = mybir.dt.uint8
FP8X4 = mybir.dt.float8_e4m3fn_x4
ALU = mybir.AluOpType
ACT = mybir.ActivationFunctionType
AX = mybir.AxisListType

P = 128
TILES = T // P


def tile_rankwisemoloradenserouter_x2_kernel(
    tc, x, w0_words, w0_scales, wr_words, wr_scales, br, a_words, a_scales, b_words, b_scales,
    out_0, out_1, out_2,
):
    nc = tc.nc
    with ExitStack() as ctx:
        const = ctx.enter_context(tc.tile_pool(name="const", bufs=1))
        keep = ctx.enter_context(tc.tile_pool(name="keep", bufs=TILES))
        four = ctx.enter_context(tc.tile_pool(name="four", bufs=4))
        psum_t = ctx.enter_context(tc.psum_pool(name="psum_t", bufs=3))
        psum_u = ctx.enter_context(tc.psum_pool(name="psum_u", bufs=2))
        psum_y = ctx.enter_context(tc.psum_pool(name="psum_y", bufs=3))
        ctx.enter_context(tc.manual_schedule())

        ident = const.tile([P, P], F32, name="ident")
        ones = const.tile([P, P], BF16, name="ones", align_bytes=64)
        br_row = const.tile([P, E], BF16, name="br_row", align_bytes=64)
        br_all = const.tile([P, E], F32, name="br_all")
        warm = const.tile([P, 1], F32, name="warm")
        w0_c = const.tile([P, 2, F], U32, name="w0_c", align_bytes=64)
        w0_s = const.tile([P, 2, F], U8, name="w0_s", align_bytes=64)
        wr_c = const.tile([P, 2, E], U32, name="wr_c", align_bytes=64)
        wr_s = const.tile([P, 2, E], U8, name="wr_s", align_bytes=64)
        a_c = const.tile([P, 2, R], U32, name="a_c", align_bytes=64)
        a_s = const.tile([P, 2, R], U8, name="a_s", align_bytes=64)
        b_c = const.tile([P, 1, F], U32, name="b_c", align_bytes=64)
        b_s = const.tile([P, 1, F], U8, name="b_s", align_bytes=64)
        y_s = const.tile([P, 2, 4 * P], U8, name="y_s", align_bytes=64)
        y_s2 = const.tile([P, 2, 4 * P], U8, name="y_s2", align_bytes=64)

        xs, xd, xg, xc, xp, xt_ps = {}, {}, {}, {}, {}, {}
        lt, ln, mn, sm, pe, rc = {}, {}, {}, {}, {}, {}
        ups, zb, zt_ps, zg, zc, zs = {}, {}, {}, {}, {}, {}
        yps, yo, yb, yt_ps, yg, yc = {}, {}, {}, {}, {}, {}

        def load_x(lo, hi):
            tiles = const.tile([P, hi - lo, D], BF16, name="x_in%d" % lo, align_bytes=64)
            nc.sync.dma_start(out=tiles[:], in_=x[P * lo : P * hi, :].rearrange("(i p) d -> p i d", p=P))
            for i in range(lo, hi):
                xs[i] = tiles[:, i - lo, :]

        def load_words(dst, src, g=None):
            if g is None:
                nc.sync.dma_start(
                    out=dst[:].bitcast(I32), in_=src.rearrange("g p n t -> p g (n t)").bitcast(I32)
                )
            else:
                nc.sync.dma_start(
                    out=dst[:, g, :].bitcast(I32), in_=src[g].rearrange("p n t -> p (n t)").bitcast(I32)
                )

        def load_scales(queue, dst, src):
            for q in range(4):
                queue.dma_start(
                    out=dst[32 * q : 32 * q + 4].bitcast(I32),
                    in_=src[:, 4 * q : 4 * q + 4, :].rearrange("g r n -> r g n").bitcast(I32),
                )

        nc.vector.memset(br_row[:], 0.0)
        nc.vector.memset(wr_s[:].rearrange("p g n -> p (g n)").bitcast(I32), 0)
        nc.vector.memset(a_s[:].rearrange("p g n -> p (g n)").bitcast(I32), 0)
        nc.vector.memset(w0_s[:].rearrange("p g n -> p (g n)").bitcast(I32), 0)
        nc.vector.memset(b_s[:].rearrange("p g n -> p (g n)").bitcast(I32), 0)
        nc.vector.memset(ones[:], 1.0)
        nc.vector.memset(warm[:], 0.0)
        make_identity(nc, ident[:])

        nc.gpsimd.dma_start(out=br_row[0:1, :], in_=br.unsqueeze(0))
        load_x(0, 1)
        load_words(wr_c, wr_words)
        load_scales(nc.sync, wr_s, wr_scales)
        load_x(1, 4)
        load_x(4, 6)
        load_x(6, 8)
        load_words(a_c, a_words)
        load_scales(nc.sync, a_s, a_scales)
        load_words(w0_c, w0_words, 0)
        load_words(w0_c, w0_words, 1)
        load_scales(nc.sync, w0_s, w0_scales)
        load_words(b_c, b_words)
        load_scales(nc.sync, b_s, b_scales)
        nc.scalar.activation(out=warm[:], in_=warm[:], func=ACT.Exp)

        def move(engine, dst, src):
            if engine == "s":
                nc.scalar.copy(out=dst, in_=src)
            else:
                nc.vector.tensor_copy(out=dst, in_=src)

        def x_split(i):
            xd[i] = keep.tile([P, D], BF16, name="xd", align_bytes=64)
            nc.vector.tensor_copy(
                out=xd[i][:].bitcast(F32).rearrange("r (g u p) -> r g u p", g=2, u=2),
                in_=xs[i].bitcast(F32).rearrange("r (g p u) -> r g u p", g=2, u=2),
            )

        def x_turn(i):
            xt_ps[i] = psum_t.tile([P, 4, P], F32, name="t_ps", tag="t_ps")
            for g in range(2):
                for u in range(2):
                    if i in xd:
                        words = xd[i][:].bitcast(F32)[:, P * (2 * g + u) : P * (2 * g + u + 1)]
                    else:
                        words = xs[i].bitcast(F32)[:, 256 * g + u : 256 * (g + 1) : 2]
                    nc.tensor.transpose(xt_ps[i][:, 2 * g + u, :], words, ident[:])

        def x_out(i, engine):
            xg[i] = keep.tile([P, 8 * P], BF16, name="xg", align_bytes=64)
            dst = xg[i][:].bitcast(F32).rearrange("p (g r u) -> p g r u", g=2, u=2)
            src = xt_ps[i][:].rearrange("p (g u) r -> p g r u", g=2)
            move(engine, dst, src)

        def x_quant(i):
            xc[i] = keep.tile([P, 2 * P], U32, name="xc", align_bytes=64)
            xp[i] = keep.tile([P, 2 * P], U8, name="xp", align_bytes=64)
            nc.vector.quantize_mx(out=xc[i][:].bitcast(FP8X4), scales=xp[i][:], in_=xg[i][:])

        def by_x(i, g, out, wc, ws, cols, start, stop):
            nc.tensor.matmul_mx(
                out=out,
                lhsT=xc[i][:, P * g : P * (g + 1)].bitcast(FP8X4),
                lhsT_scale=xp[i][:, P * g : P * (g + 1)],
                rhs=wc[:, g, cols].bitcast(FP8X4),
                rhs_scale=ws[:, g, cols],
                start=start,
                stop=stop,
            )

        def logits(b):
            lt[b] = psum_y.tile([P, 4, P], F32, name="l_ps", tag="y_ps")
            for j in range(2):
                for g in range(2):
                    by_x(2 * b + j, g, lt[b][:, j, :], wr_c, wr_s, slice(0, E), g == 0, g == 1)

        def soft_a(b):
            ln[b] = four.tile([P, 2, E], F32, name="ln")
            mn[b] = four.tile([P, 2], F32, name="mn")
            nc.vector.scalar_tensor_tensor(
                out=ln[b][:], in0=lt[b][:, 0:2, :], scalar=-1.0, op0=ALU.mult,
                in1=br_all[:].unsqueeze(1).to_broadcast([P, 2, E]), op1=ALU.subtract,
            )
            nc.vector.tensor_reduce(out=mn[b][:], in_=ln[b][:], axis=AX.X, op=ALU.min)

        def soft_b(b):
            pe[b] = four.tile([P, 2, E], F32, name="pe")
            sm[b] = four.tile([P, 2], F32, name="sm")
            for j in range(2):
                nc.scalar.activation(
                    out=pe[b][:, j, :], in_=ln[b][:, j, :], func=ACT.Exp,
                    bias=mn[b][:, j : j + 1], scale=-1.0, accum_out=sm[b][:, j : j + 1],
                )

        def soft_c(b):
            sc = four.tile([P, 2], F32, name="sc")
            rc[b] = four.tile([P, 2], F32, name="rc")
            nc.vector.tensor_scalar(out=sc[:], in0=sm[b][:], scalar1=1.0 / E, scalar2=None, op0=ALU.mult)
            nc.vector.reciprocal(out=rc[b][:], in_=sc[:])

        def down(i):
            ups[i] = psum_u.tile([P, R], F32, name="u_ps")
            for g in range(2):
                by_x(i, g, ups[i][:], a_c, a_s, slice(0, R), g == 0, g == 1)

        def gate(i):
            b, j = i // 2, i % 2
            if j == 0:
                zb[b] = four.tile([P, 2, R], BF16, name="zb", align_bytes=64)
            src = ups[i][:].rearrange("q (p u e) -> q u p e", u=2, e=2)
            dst = zb[b][:, j, :].rearrange("q (u p e) -> q u p e", u=2, e=2)
            for u in range(2):
                nc.vector.scalar_tensor_tensor(
                    out=dst[:, u], in0=src[:, u], scalar=rc[b][:, j : j + 1], op0=ALU.mult,
                    in1=pe[b][:, j, :].unsqueeze(2).to_broadcast([P, E, 2]), op1=ALU.mult,
                )

        def z_turn(b):
            zt_ps[b] = psum_t.tile([P, 4, P], F32, name="z_ps", tag="t_ps")
            words = zb[b][:].rearrange("q j k -> q (j k)").bitcast(F32)
            for k in range(4):
                nc.tensor.transpose(zt_ps[b][:, k, :], words[:, P * k : P * (k + 1)], ident[:])

        def z_out(b, engine):
            zg[b] = four.tile([P, 8 * P], BF16, name="zg", align_bytes=64)
            move(
                engine,
                zg[b][:].bitcast(F32).rearrange("p (j r u) -> p j r u", j=2, u=2),
                zt_ps[b][:].rearrange("p (j u) r -> p j r u", j=2),
            )

        def z_quant(b):
            zc[b] = four.tile([P, 2 * P], U32, name="zc", align_bytes=64)
            zs[b] = four.tile([P, 2 * P], U8, name="zs", align_bytes=64)
            nc.vector.quantize_mx(out=zc[b][:].bitcast(FP8X4), scales=zs[b][:], in_=zg[b][:])

        def base(i, h):
            if h == 0:
                yo[i] = keep.tile([P, F], F32, name="yo")
                yb[i] = keep.tile([P, F], BF16, name="yb", align_bytes=64)
            yps[i, h] = psum_y.tile([P, 512], F32, name="y_ps", tag="y_ps")
            for g in range(2):
                by_x(i, g, yps[i, h][:], w0_c, w0_s, slice(512 * h, 512 * (h + 1)), g == 0, False)

        def up(i, h):
            cols = slice(512 * h, 512 * (h + 1))
            nc.tensor.matmul_mx(
                out=yps[i, h][:],
                lhsT=zc[i // 2][:, P * (i % 2) : P * (i % 2 + 1)].bitcast(FP8X4),
                lhsT_scale=zs[i // 2][:, P * (i % 2) : P * (i % 2 + 1)],
                rhs=b_c[:, 0, cols].bitcast(FP8X4), rhs_scale=b_s[:, 0, cols],
                start=False, stop=True,
            )

        def y_out(i, h, engine):
            move(engine, yo[i][:, 512 * h : 512 * (h + 1)], yps[i, h][:])

        def y_store(i, h=None):
            cols = slice(0, F) if h is None else slice(512 * h, 512 * (h + 1))
            nc.sync.dma_start(out=out_0[P * i : P * (i + 1), cols], in_=yo[i][:, cols])

        def y_round(i, h):
            cols = slice(512 * h, 512 * (h + 1))
            nc.vector.tensor_copy(
                out=yb[i][:, cols].rearrange("q (u p e) -> q u p e", u=2, e=2),
                in_=yo[i][:, cols].rearrange("q (p u e) -> q u p e", u=2, e=2),
            )

        def y_turn(i):
            yt_ps[i] = psum_t.tile([P, 4, P], F32, name="yt_ps", tag="t_ps")
            words = yb[i][:].bitcast(F32)
            for k in range(4):
                nc.tensor.transpose(yt_ps[i][:, k, :], words[:, P * k : P * (k + 1)], ident[:])

        def yt_out(i, engine):
            yg[i] = keep.tile([P, 8 * P], BF16, name="yg", align_bytes=64)
            move(
                engine,
                yg[i][:].bitcast(F32).rearrange("p (h r u) -> p h r u", h=2, u=2),
                yt_ps[i][:].rearrange("p (h u) r -> p h r u", h=2),
            )

        def plane(i):
            return y_s if i < 4 else y_s2

        def y_quant(i):
            for h in range(2):
                quantize_half(i, h, yg[i][:, 512 * h : 512 * (h + 1)])

        def quantize_half(i, h, values):
            first = i if i >= 6 else i - i % 2
            if first not in yc:
                yc[first] = four.tile([P, 2, P if i >= 6 else 2 * P], U32, name="yc%d" % (i // 6), align_bytes=64)
            nc.vector.quantize_mx(
                out=yc[first][:, h, P * (i - first) : P * (i - first + 1)].bitcast(FP8X4),
                scales=plane(i)[:, h, P * (i % 4) : P * (i % 4 + 1)],
                in_=values,
            )

        def words_store(lo, hi):
            nc.sync.dma_start(
                out=out_1[:, :, P * lo : P * hi, :].rearrange("h p r t -> p h (r t)").bitcast(I32),
                in_=yc[lo][:].bitcast(I32),
            )

        def scales_store(lo, hi, queues):
            for q in range(4):
                {"s": nc.scalar, "y": nc.sync, "p": nc.gpsimd}[queues[q]].dma_start(
                    out=out_2[:, 4 * q : 4 * q + 4, P * lo : P * hi].rearrange("h r n -> r h n").bitcast(I32),
                    in_=plane(lo)[32 * q : 32 * q + 4].bitcast(I32),
                )

        def y_round_ps(i, h):
            nc.vector.tensor_copy(
                out=yb[i][:, 512 * h : 512 * (h + 1)].rearrange("q (u p e) -> q u p e", u=2, e=2),
                in_=yps[i, h][:].rearrange("q (p u e) -> q u p e", u=2, e=2),
            )

        def half_turn(i, h):
            yt_ps[i, h] = psum_t.tile([P, 4, P], F32, name="yt_ps", tag="t_ps")
            words = yb[i][:].bitcast(F32)
            for u in range(2):
                k = 2 * h + u
                nc.tensor.transpose(yt_ps[i, h][:, u, :], words[:, P * k : P * (k + 1)], ident[:])

        def half_out(i, h, engine):
            yg[i, h] = keep.tile([P, 4 * P], BF16, name="ygh", align_bytes=64)
            move(
                engine,
                yg[i, h][:].bitcast(F32).rearrange("p (r u) -> p r u", u=2),
                yt_ps[i, h][:, 0:2, :].rearrange("p u r -> p r u"),
            )

        def half_quant(i, h):
            quantize_half(i, h, yg[i, h][:])

        def half_y_store(i, h):
            cols = slice(512 * h, 512 * (h + 1))
            nc.sync.dma_start(out=out_0[P * i : P * (i + 1), cols], in_=yo[i][:, cols])

        def bias():
            lt["br"] = psum_y.tile([P, 4, P], F32, name="br_ps", tag="y_ps")
            nc.tensor.matmul(out=lt["br"][:, 0, :], lhsT=ones[:], rhs=br_row[:], start=True, stop=True)

        def bias_out():
            nc.vector.tensor_copy(out=br_all[:], in_=lt["br"][:, 0, :])

        x_turn(0)
        x_turn(1)
        x_out(0, "v")
        bias()
        x_split(2)
        x_quant(0)
        x_out(1, "s")
        x_split(3)
        x_turn(2)
        x_out(2, "s")
        bias_out()
        x_turn(3)
        x_split(4)
        x_split(5)
        x_quant(1)
        x_out(3, "s")
        logits(0)
        x_quant(2)
        x_split(6)
        x_quant(3)
        x_turn(4)
        logits(1)
        x_split(7)
        x_out(4, "s")
        soft_a(0)
        x_turn(5)
        down(0)
        x_turn(6)
        down(1)
        x_quant(4)
        x_out(5, "s")
        soft_b(0)
        x_out(6, "s")
        soft_a(1)
        soft_c(0)
        x_quant(5)
        gate(0)
        gate(1)
        x_turn(7)
        soft_b(1)
        logits(2)
        down(2)
        soft_c(1)
        gate(2)
        soft_a(2)
        z_turn(0)
        down(3)
        z_out(0, "s")
        base(0, 0)
        base(0, 1)
        gate(3)
        z_quant(0)
        base(1, 0)
        soft_b(2)
        down(4)
        x_quant(6)
        down(5)
        x_out(7, "s")
        soft_c(2)
        x_quant(7)
        up(0, 0)
        up(0, 1)
        gate(4)
        y_out(0, 0, "s")
        up(1, 0)
        y_out(0, 1, "s")
        z_turn(1)
        base(1, 1)
        up(1, 1)
        logits(3)
        z_out(1, "v")
        y_out(1, 0, "s")
        y_round(0, 0)
        down(6)
        gate(5)
        y_out(1, 1, "s")
        base(2, 0)
        base(2, 1)
        z_quant(1)
        soft_a(3)
        y_round(0, 1)
        up(2, 0)
        base(3, 0)
        y_round(1, 0)
        y_out(2, 0, "s")
        y_round(1, 1)
        y_round(2, 0)
        y_store(0)
        soft_b(3)
        soft_c(3)
        up(2, 1)
        y_turn(0)
        y_turn(1)
        y_out(2, 1, "s")
        z_turn(2)
        yt_out(0, "s")
        up(3, 0)
        z_out(2, "v")
        base(3, 1)
        yt_out(1, "s")
        down(7)
        y_out(3, 0, "s")
        y_round(2, 1)
        y_quant(0)
        gate(6)
        up(3, 1)
        y_out(3, 1, "s")
        z_quant(2)
        base(4, 0)
        base(4, 1)
        up(4, 0)
        y_out(4, 0, "s")
        up(4, 1)
        y_round(3, 0)
        gate(7)
        z_turn(3)
        y_out(4, 1, "s")
        y_round(3, 1)
        y_store(1)
        y_turn(2)
        z_out(3, "v")
        y_store(2)
        y_round(4, 0)
        yt_out(2, "s")
        y_quant(1)
        y_turn(3)
        base(5, 0)
        y_store(3)
        y_quant(2)
        y_round(4, 1)
        yt_out(3, "s")
        y_store(4)
        up(5, 0)
        z_quant(3)
        words_store(0, 2)
        base(5, 1)
        y_quant(3)
        base(6, 0)
        y_out(5, 0, "s")
        up(5, 1)
        y_round(5, 0)
        y_out(5, 1, "s")
        up(6, 0)
        base(6, 1)
        up(6, 1)
        y_out(6, 0, "v")
        words_store(2, 4)
        y_turn(4)
        base(7, 0)
        up(7, 0)
        y_round(5, 1)
        yt_out(4, "s")
        y_out(6, 1, "v")
        y_round(6, 0)
        base(7, 1)
        scales_store(0, 4, "yyyy")
        up(7, 1)
        y_turn(5)
        y_out(7, 0, "s")
        y_round(6, 1)
        y_store(5)
        y_turn(6)
        y_quant(4)
        y_round(7, 0)
        y_store(6)
        y_round_ps(7, 1)
        half_turn(7, 0)
        half_y_store(7, 0)
        yt_out(5, "s")
        half_turn(7, 1)
        half_out(7, 0, "v")
        yt_out(6, "s")
        y_quant(5)
        half_out(7, 1, "s")
        half_quant(7, 0)
        y_out(7, 1, "s")
        words_store(4, 6)
        y_quant(6)
        half_quant(7, 1)
        words_store(6, 7)
        scales_store(4, 8, "sysy")
        half_y_store(7, 1)
        words_store(7, 8)
